import numpy as np
import ml_dtypes


def mxq(x, axis, fmt="e4m3"):
    dtype, down = {"e4m3": (ml_dtypes.float8_e4m3fn, 7), "e5m2": (ml_dtypes.float8_e5m2, 14)}[fmt]
    v = np.moveaxis(np.asarray(x, np.float32).astype(ml_dtypes.bfloat16).astype(np.float64), axis, -1)
    blocks = v.reshape(v.shape[:-1] + (-1, 32))
    amax = np.abs(blocks).max(-1, keepdims=True)
    byte = np.maximum(np.where(amax > 0, np.frexp(amax)[1] - 1 + 127, 0) - down, 1)
    scale = np.exp2(byte - 127.0)
    codes = (blocks / scale).astype(np.float32).astype(dtype).astype(np.float64)
    return np.moveaxis((codes * scale).reshape(v.shape), -1, axis)


WIDE = False


def mx_kscale(k):
    if not WIDE:
        return np.ones(k)
    levels = np.array([10, -10, 5, -5, 0])
    if k % 512:
        return np.exp2(np.random.permutation(np.resize(levels, k // 32))).repeat(32)
    a = np.empty((k // 512, 16))
    for p in range(k // 512):
        a[p, :8] = np.random.permutation(np.resize(levels, 8))
        for g in range(8):
            far = levels[np.abs(levels - a[p, g]) >= 10]
            a[p, g + 8] = far[np.random.randint(len(far))]
    return np.exp2(a.ravel()).repeat(32)


BF16 = ml_dtypes.bfloat16


def bf(x):
    return np.asarray(x, np.float32).astype(BF16)


def f64(x):
    return np.asarray(x).astype(np.float64)

def planes(Y):
    n, m = Y.shape
    b = f64(bf(Y)).reshape(n // 32, 32, m)
    amax = np.abs(b).max(1)
    byte = np.clip(np.where(amax > 0, np.frexp(amax)[1] - 1 + 127 - 7, 1), 1, 254)
    codes = (b * np.exp2(127.0 - byte)[:, None, :]).reshape(n, m).astype(np.float32).astype(ml_dtypes.float8_e4m3fn).view(np.uint8)
    words = codes.reshape(n // 512, 128, 4, m).transpose(0, 1, 3, 2)
    return np.ascontiguousarray(words), np.ascontiguousarray(byte.astype(np.uint8).reshape(n // 512, 16, m))


TRIALS, CH, L, N = 32, 32, 1024, 2048

OMEGA = 5.0

def morlet_bank():
    centre = L * np.random.rand(N)
    width = L * 2.0 ** (-2.0 - 3.0 * np.random.rand(N))
    u = (np.arange(L)[:, None] - centre) / width
    atoms = np.cos(OMEGA * u) * np.exp(-0.5 * u * u)
    return atoms / np.sqrt((atoms * atoms).sum(axis=0))

def setup_inputs():
    s = mx_kscale(L)
    x = np.random.randn(TRIALS, CH, L)
    size = np.exp(0.8 * np.random.randn(N))
    analysis = (morlet_bank() + 0.5 * np.random.randn(L, N) / np.sqrt(L)) * size
    lam_sq = (0.6 * size * np.exp(0.2 * np.random.randn(N))) ** 2
    return {"x": bf(x * s), "analysis": bf(analysis / s[:, None]), "lam_sq": bf(lam_sq)}

def reference(x, analysis, lam_sq):
    xq = mxq(f64(x).reshape(TRIALS * CH, L), 1, "e4m3")
    aq = mxq(f64(analysis), 0, "e4m3")
    c = xq @ aq
    e = c * c
    gain = e / (e + f64(lam_sq))
    y = (c * gain).reshape(TRIALS, CH, N)
    words, scales = planes(y.reshape(TRIALS * CH, N).T)
    return y, words, scales

@@ -1,0 +1,359 @@
+from contextlib import ExitStack
+
+import concourse.mybir as mybir
+from concourse.masks import make_identity
+
+M, K, N = 1024, 1024, 2048
+FLOPS = 2 * M * K * N
+
+F32 = mybir.dt.float32
+BF16 = mybir.dt.bfloat16
+I32 = mybir.dt.int32
+U32 = mybir.dt.uint32
+U8 = mybir.dt.uint8
+FP8X4 = mybir.dt.float8_e4m3fn_x4
+ACT = mybir.ActivationFunctionType
+MULT = mybir.AluOpType.mult
+
+P = 128
+PACK = 4
+K_PASS = P * PACK
+PASSES = K // K_PASS
+GROUP = P * PACK
+GROUPS = N // GROUP
+MW = 256
+QUARTERS = M // MW
+UNITS = GROUPS * QUARTERS
+ITEMS = 2 * UNITS
+BANK = 512
+C_BANKS = 5
+T_BANKS = 3
+RING = 3
+OUT_RING = 6
+
+
+def tile_morlet_coefficient_shrinkage_g1_kernel(tc, x, analysis, lam_sq, out_0, out_1, out_2):
+    nc = tc.nc
+    x2 = x.rearrange("a b k -> (a b) k")
+    y2 = out_0.rearrange("a b n -> (a b) n")
+    words_hbm = out_1.rearrange("g p m t -> g p (m t)").bitcast(I32)
+    scales_hbm = out_2.bitcast(I32)
+
+    with ExitStack() as ctx:
+        sb = ctx.enter_context(tc.tile_pool(name="sb", bufs=1))
+        ps = ctx.enter_context(tc.psum_pool(name="ps", bufs=1))
+        ctx.enter_context(tc.manual_schedule())
+
+        ident = sb.tile([P, P], F32, name="ident")
+        warm = sb.tile([P, 16], F32, name="warm")
+        lam = sb.tile([P, GROUPS, PACK], BF16, name="lam")
+        x_raw = sb.tile([P, M // P, K], BF16, name="x_raw")
+        a_raw = sb.tile([P, GROUPS, PASSES, PACK, GROUP], BF16, name="a_raw")
+        x_stage = sb.tile([P, QUARTERS - 1, PASSES * MW * PACK], BF16, name="x_stage", align_bytes=64)
+        a_stage = sb.tile([P, 3, GROUP * PACK], BF16, name="a_stage", align_bytes=64)
+        g_stage = sb.tile([P, 2 * GROUP * PACK], BF16, name="g_stage", align_bytes=64)
+        tail_stage = sb.tile([P, 2 * MW * PACK], BF16, name="tail_stage", align_bytes=64)
+        x_codes = sb.tile([P, QUARTERS, PASSES * MW], U32, name="x_codes", align_bytes=64)
+        x_scales = sb.tile([P, QUARTERS, PASSES * MW], U8, name="x_scales", align_bytes=64)
+        a_codes = sb.tile([P, GROUPS, PASSES, GROUP], U32, name="a_codes", align_bytes=64)
+        a_scales = sb.tile([P, GROUPS, PASSES, GROUP], U8, name="a_scales", align_bytes=64)
+        y_codes = sb.tile([P, GROUPS * M], U32, name="y_codes", align_bytes=64)
+        y_scales = sb.tile([P, GROUPS * M], U8, name="y_scales", align_bytes=64)
+        e_t = sb.tile([P, RING, BANK], F32, name="e_t")
+        r_t = sb.tile([P, RING, BANK], F32, name="r_t")
+        u_t = sb.tile([P, RING, BANK], F32, name="u_t")
+        g_t = sb.tile([P, RING, BANK], F32, name="g_t")
+        y_t = sb.tile([P, UNITS, PACK, MW], F32, name="y_t")
+        o_t = sb.tile([P, OUT_RING, BANK], F32, name="o_t")
+        c_bank = [ps.tile([P, BANK], F32, name="c_bank%d" % b) for b in range(C_BANKS)]
+        t_bank = [ps.tile([P, BANK], F32, name="t_bank%d" % b) for b in range(T_BANKS)]
+
+        def copy(engine, out, in_):
+            if engine == "s":
+                nc.scalar.copy(out=out, in_=in_)
+            elif engine == "v":
+                nc.vector.tensor_copy(out=out, in_=in_)
+            else:
+                nc.gpsimd.tensor_scalar(out=out, in0=in_, scalar1=1.0, scalar2=1.0, op0=MULT, op1=MULT)
+
+        def load_x(b0, b1):
+            nc.sync.dma_start(
+                out=x_raw[:, b0:b1, :], in_=x2[b0 * P : b1 * P, :].rearrange("(b p) k -> p b k", p=P)
+            )
+
+        def load_a(g, j):
+            rows = analysis[j * K_PASS : (j + 1) * K_PASS, g * GROUP : (g + 1) * GROUP]
+            nc.sync.dma_start(out=a_raw[:, g, j, :, :], in_=rows.rearrange("(p r) n -> p r n", r=PACK))
+
+        def x_stage_of(q):
+            return x_stage[:, q, :] if q < QUARTERS - 1 else g_stage[:, 0 : GROUP * PACK]
+
+        def turn_x(b):
+            words = x_raw[:, b, :].bitcast(F32)
+            bank = t_bank[b % T_BANKS]
+            for j in range(PASSES):
+                for h in range(2):
+                    col = (2 * j + h) * P
+                    nc.tensor.transpose(
+                        bank[:, col : col + P], words[:, 256 * j + h : 256 * (j + 1) : 2], ident[:]
+                    )
+
+        def copy_x(engine, b):
+            dst = x_stage_of(b // 2).bitcast(F32).rearrange("p (j m h) -> p j m h", j=PASSES, h=2)
+            half = b % 2
+            copy(
+                engine,
+                dst[:, :, half * P : (half + 1) * P, :],
+                t_bank[b % T_BANKS][:].rearrange("p (j h m) -> p j m h", j=PASSES, h=2),
+            )
+
+        def quantize(codes, scales, src):
+            nc.vector.quantize_mx(out=codes.bitcast(FP8X4), scales=scales, in_=src)
+
+        def quant_x(q):
+            quantize(x_codes[:, q, :], x_scales[:, q, :], x_stage_of(q))
+
+        def weave_a(engine, g, j, t0, t1, stage):
+            src = a_raw[:, g, j, :, :].rearrange("p r (c t) -> p t c r", t=PACK)
+            dst = stage.rearrange("p (t c r) -> p t c r", t=PACK, r=PACK)
+            copy(engine, dst[:, t0:t1], src[:, t0:t1])
+
+        def quant_a(g, j, t0, t1, stage):
+            cols = slice(t0 * P, t1 * P)
+            quantize(a_codes[:, g, j, cols], a_scales[:, g, j, cols], stage[:, t0 * GROUP : t1 * GROUP])
+
+        def multiply(i):
+            g, q = divmod(i // 2, QUARTERS)
+            for tt in range(2):
+                t = 2 * (i % 2) + tt
+                for j in range(PASSES):
+                    nc.tensor.matmul_mx(
+                        out=c_bank[i % C_BANKS][:, tt * MW : (tt + 1) * MW],
+                        lhsT=a_codes[:, g, j, t * P : (t + 1) * P].bitcast(FP8X4),
+                        lhsT_scale=a_scales[:, g, j, t * P : (t + 1) * P],
+                        rhs=x_codes[:, q, j * MW : (j + 1) * MW].bitcast(FP8X4),
+                        rhs_scale=x_scales[:, q, j * MW : (j + 1) * MW],
+                        start=(j == 0),
+                        stop=(j == PASSES - 1),
+                    )
+
+        def square_c(i):
+            nc.scalar.activation(out=e_t[:, i % RING, :], in_=c_bank[i % C_BANKS][:], func=ACT.Square)
+
+        def rsqrt(i):
+            g = i // (2 * QUARTERS)
+            for tt in range(2):
+                t = 2 * (i % 2) + tt
+                cols = slice(tt * MW, (tt + 1) * MW)
+                nc.scalar.activation(
+                    out=r_t[:, i % RING, cols],
+                    in_=e_t[:, i % RING, cols],
+                    func=ACT.Abs_reciprocal_sqrt,
+                    bias=lam[:, g, t : t + 1],
+                )
+
+        def ratio(i):
+            nc.vector.tensor_tensor(
+                out=u_t[:, i % RING, :], in0=c_bank[i % C_BANKS][:], in1=r_t[:, i % RING, :], op=MULT
+            )
+
+        def gain(i):
+            nc.scalar.activation(out=g_t[:, i % RING, :], in_=u_t[:, i % RING, :], func=ACT.Square)
+
+        def shrink(i):
+            t = 2 * (i % 2)
+            nc.vector.tensor_tensor(
+                out=y_t[:, i // 2, t : t + 2, :].rearrange("p t m -> p (t m)"),
+                in0=c_bank[i % C_BANKS][:],
+                in1=g_t[:, i % RING, :],
+                op=MULT,
+            )
+
+        def out_bank(block):
+            return t_bank[(M // P + block) % T_BANKS]
+
+        def turn_y(unit):
+            for half in range(2):
+                bank = out_bank(2 * unit + half)
+                for t in range(PACK):
+                    nc.tensor.transpose(
+                        bank[:, t * P : (t + 1) * P], y_t[:, unit, t, half * P : (half + 1) * P], ident[:]
+                    )
+
+        def store_y(engine, block):
+            g, b = divmod(block, M // P)
+            dst = o_t[:, block % OUT_RING, :]
+            copy(
+                engine,
+                dst.rearrange("m (p t) -> m p t", t=PACK),
+                out_bank(block)[:].rearrange("m (t p) -> m p t", t=PACK),
+            )
+            nc.sync.dma_start(out=y2[b * P : (b + 1) * P, g * GROUP : (g + 1) * GROUP], in_=dst)
+
+        def round_y(engine, u0, u1, stage):
+            copy(
+                engine,
+                stage.rearrange("p (u m t) -> p u m t", m=MW, t=PACK),
+                y_t[:, u0:u1].rearrange("p u t m -> p u m t"),
+            )
+
+        def quant_y(u0, u1, stage):
+            quantize(y_codes[:, u0 * MW : u1 * MW], y_scales[:, u0 * MW : u1 * MW], stage)
+
+        def store_words(u0, u1):
+            for g in range(GROUPS):
+                lo, hi = max(u0, g * QUARTERS), min(u1, (g + 1) * QUARTERS)
+                if lo < hi:
+                    nc.sync.dma_start(
+                        out=words_hbm[g, :, (lo - g * QUARTERS) * MW : (hi - g * QUARTERS) * MW],
+                        in_=y_codes[:, lo * MW : hi * MW].bitcast(I32),
+                    )
+
+        def store_scales(g0, g1):
+            plane = y_scales[:].bitcast(I32).rearrange("p (g w) -> p g w", g=GROUPS)
+            for quad in range(4):
+                nc.sync.dma_start(
+                    out=scales_hbm[g0:g1, 4 * quad : 4 * quad + 4, :].rearrange("g r w -> r g w"),
+                    in_=plane[32 * quad : 32 * quad + 4, g0:g1, :],
+                )
+
+        W = GROUP * PACK
+        lower, upper = g_stage[:, 0:W], g_stage[:, W : 2 * W]
+        UW = MW * PACK
+
+        nc.vector.memset(warm[:, 0:1], 1.0)
+        nc.scalar.activation(out=warm[:, 8:9], in_=warm[:, 0:1], func=ACT.Abs_reciprocal_sqrt)
+        load_x(0, 1)
+        load_x(1, 2)
+        load_a(0, 0)
+        load_a(0, 1)
+        with nc.allow_non_contiguous_dma(reason="four thresholds to a partition and group"):
+            nc.scalar.dma_start(out=lam[:], in_=lam_sq.rearrange("(g p t) -> p g t", p=P, t=PACK))
+        for b in (2, 4, 6):
+            load_x(b, b + 2)
+        for g in range(1, GROUPS):
+            for j in range(PASSES):
+                load_a(g, j)
+        make_identity(nc, ident[:])
+
+        turn_x(0)
+        turn_x(1)
+        copy_x("s", 0)
+        copy_x("s", 1)
+        turn_x(2)
+        turn_x(3)
+        weave_a("v", 0, 0, 0, 2, a_stage[:, 0, :])
+        weave_a("s", 0, 0, 2, 4, a_stage[:, 0, :])
+        weave_a("s", 0, 1, 2, 4, a_stage[:, 1, :])
+        quant_x(0)
+        quant_a(0, 0, 0, 2, a_stage[:, 0, :])
+        weave_a("v", 0, 1, 0, 2, a_stage[:, 1, :])
+        quant_a(0, 0, 2, 4, a_stage[:, 0, :])
+        quant_a(0, 1, 0, 2, a_stage[:, 1, :])
+        multiply(0)
+        copy_x("v", 2)
+        quant_a(0, 1, 2, 4, a_stage[:, 1, :])
+        multiply(1)
+        copy_x("v", 3)
+        quant_x(1)
+
+        def slot(s):
+            if s == 2:
+                quant_x(2)
+            elif s == 3:
+                quant_x(3)
+                weave_a("g", 1, 1, 0, 4, lower)
+                weave_a("g", 2, 0, 0, 4, upper)
+            elif s == 7:
+                quant_a(1, 0, 0, 4, a_stage[:, 2, :])
+                quant_a(1, 1, 0, 4, lower)
+                quant_a(2, 0, 0, 4, upper)
+                weave_a("g", 2, 1, 0, 4, upper)
+                round_y("g", 0, 1, lower[:, 0:UW])
+            elif s == 11:
+                quant_a(2, 1, 0, 4, upper)
+                quant_y(0, 1, lower[:, 0:UW])
+                store_words(0, 1)
+                weave_a("g", 3, 0, 0, 4, lower)
+                round_y("g", 1, 2, upper[:, 0:UW])
+            elif s == 15:
+                quant_a(3, 0, 0, 4, lower)
+                quant_y(1, 2, upper[:, 0:UW])
+                store_words(1, 2)
+                weave_a("g", 3, 1, 0, 4, upper)
+                round_y("g", 2, 3, lower[:, 0:UW])
+            elif s == 19:
+                quant_a(3, 1, 0, 4, upper)
+                quant_y(2, 3, lower[:, 0:UW])
+                store_words(2, 3)
+                round_y("g", 3, 6, g_stage[:, 0 : 3 * UW])
+            elif s in (23, 27, 31):
+                u0 = 3 + 3 * ((s - 23) // 4)
+                quant_y(u0, u0 + 2, g_stage[:, 0 : 2 * UW])
+                quant_y(u0 + 2, u0 + 3, g_stage[:, 2 * UW : 3 * UW])
+                store_words(u0, u0 + 3)
+                u1 = min(u0 + 6, UNITS - 2)
+                round_y("g", u0 + 3, u1, g_stage[:, 0 : (u1 - u0 - 3) * UW])
+                if s == 31:
+                    store_scales(0, 3)
+
+        for s in range(ITEMS + 3):
+            slot(s)
+            if s == 0:
+                turn_x(4)
+                turn_x(5)
+            if s == 1:
+                turn_x(6)
+                turn_x(7)
+            if s >= 5 and s % 2 == 1:
+                turn_y((s - 5) // 2)
+            block = s - 6
+            if s == 2:
+                copy_x("v", 7)
+            if s == 0:
+                copy_x("v", 4)
+                copy_x("v", 5)
+            if 0 <= block and s % 8 != 3 and s < ITEMS:
+                store_y("v", block)
+            if 1 <= s <= ITEMS:
+                rsqrt(s - 1)
+            if s < ITEMS:
+                square_c(s)
+            if 2 <= s <= ITEMS + 1:
+                gain(s - 2)
+            if s == 2:
+                weave_a("s", 1, 0, 0, 2, a_stage[:, 2, :])
+            if s == 4:
+                weave_a("s", 1, 0, 2, 4, a_stage[:, 2, :])
+            if 0 <= block and s % 8 == 3 and s < ITEMS:
+                store_y("s", block)
+            if s == ITEMS:
+                store_y("s", 26)
+                store_y("s", 27)
+            if s == ITEMS + 1:
+                store_y("s", 28)
+                store_y("s", 29)
+            if s == ITEMS + 2:
+                round_y("s", 14, 15, tail_stage[:, 0:UW])
+            if s == ITEMS + 1:
+                quant_y(12, 14, g_stage[:, 0 : 2 * UW])
+                store_words(12, 14)
+            if s >= 3:
+                shrink(s - 3)
+            if 1 <= s <= ITEMS:
+                ratio(s - 1)
+            if s == 1:
+                copy_x("v", 6)
+            if s == 7:
+                multiply(8)
+            if s + 2 < ITEMS and s != 6:
+                multiply(s + 2)
+
+        turn_y(UNITS - 1)
+        quant_y(14, 15, tail_stage[:, 0:UW])
+        round_y("v", 15, 16, tail_stage[:, UW : 2 * UW])
+        store_y("s", 30)
+        store_y("s", 31)
+        quant_y(15, 16, tail_stage[:, UW : 2 * UW])
+        store_words(14, 16)
+        store_scales(3, 4)

@@ -28,8 +28,8 @@ ITEMS = 2 * UNITS
 BANK = 512
 C_BANKS = 5
 T_BANKS = 3
-RING = 3
-OUT_RING = 6
+RING = 4
+OUT_RING = 8
 
 
 def tile_morlet_coefficient_shrinkage_g1_kernel(tc, x, analysis, lam_sq, out_0, out_1, out_2):
@@ -50,9 +50,8 @@ def tile_morlet_coefficient_shrinkage_g1_kernel(tc, x, analysis, lam_sq, out_0, 
         x_raw = sb.tile([P, M // P, K], BF16, name="x_raw")
         a_raw = sb.tile([P, GROUPS, PASSES, PACK, GROUP], BF16, name="a_raw")
         x_stage = sb.tile([P, QUARTERS - 1, PASSES * MW * PACK], BF16, name="x_stage", align_bytes=64)
-        a_stage = sb.tile([P, 3, GROUP * PACK], BF16, name="a_stage", align_bytes=64)
+        a_stage = sb.tile([P, 2, GROUP * PACK], BF16, name="a_stage", align_bytes=64)
         g_stage = sb.tile([P, 2 * GROUP * PACK], BF16, name="g_stage", align_bytes=64)
-        tail_stage = sb.tile([P, 2 * MW * PACK], BF16, name="tail_stage", align_bytes=64)
         x_codes = sb.tile([P, QUARTERS, PASSES * MW], U32, name="x_codes", align_bytes=64)
         x_scales = sb.tile([P, QUARTERS, PASSES * MW], U8, name="x_scales", align_bytes=64)
         a_codes = sb.tile([P, GROUPS, PASSES, GROUP], U32, name="a_codes", align_bytes=64)
@@ -86,11 +85,14 @@ def tile_morlet_coefficient_shrinkage_g1_kernel(tc, x, analysis, lam_sq, out_0, 
             nc.sync.dma_start(out=a_raw[:, g, j, :, :], in_=rows.rearrange("(p r) n -> p r n", r=PACK))
 
         def x_stage_of(q):
-            return x_stage[:, q, :] if q < QUARTERS - 1 else g_stage[:, 0 : GROUP * PACK]
+            return g_stage[:, 0 : GROUP * PACK] if q == 3 else x_stage[:, q, :]
+
+        def x_bank(b):
+            return (t_bank + [c_bank[4], c_bank[3]] + t_bank)[b]
 
         def turn_x(b):
             words = x_raw[:, b, :].bitcast(F32)
-            bank = t_bank[b % T_BANKS]
+            bank = x_bank(b)
             for j in range(PASSES):
                 for h in range(2):
                     col = (2 * j + h) * P
@@ -104,7 +106,7 @@ def tile_morlet_coefficient_shrinkage_g1_kernel(tc, x, analysis, lam_sq, out_0, 
             copy(
                 engine,
                 dst[:, :, half * P : (half + 1) * P, :],
-                t_bank[b % T_BANKS][:].rearrange("p (j h m) -> p j m h", j=PASSES, h=2),
+                x_bank(b)[:].rearrange("p (j h m) -> p j m h", j=PASSES, h=2),
             )
 
         def quantize(codes, scales, src):
@@ -122,17 +124,23 @@ def tile_morlet_coefficient_shrinkage_g1_kernel(tc, x, analysis, lam_sq, out_0, 
             cols = slice(t0 * P, t1 * P)
             quantize(a_codes[:, g, j, cols], a_scales[:, g, j, cols], stage[:, t0 * GROUP : t1 * GROUP])
 
+        def item(i):
+            if i // 2 < UNITS - 1:
+                return range(2 * (i % 2), 2 * (i % 2) + 2), 0, MW
+            return range(PACK), (i % 2) * P, P
+
         def multiply(i):
             g, q = divmod(i // 2, QUARTERS)
-            for tt in range(2):
-                t = 2 * (i % 2) + tt
+            ts, m0, mw = item(i)
+            for tt, t in enumerate(ts):
                 for j in range(PASSES):
+                    cols = slice(j * MW + m0, j * MW + m0 + mw)
                     nc.tensor.matmul_mx(
-                        out=c_bank[i % C_BANKS][:, tt * MW : (tt + 1) * MW],
+                        out=c_bank[i % C_BANKS][:, tt * mw : (tt + 1) * mw],
                         lhsT=a_codes[:, g, j, t * P : (t + 1) * P].bitcast(FP8X4),
                         lhsT_scale=a_scales[:, g, j, t * P : (t + 1) * P],
-                        rhs=x_codes[:, q, j * MW : (j + 1) * MW].bitcast(FP8X4),
-                        rhs_scale=x_scales[:, q, j * MW : (j + 1) * MW],
+                        rhs=x_codes[:, q, cols].bitcast(FP8X4),
+                        rhs_scale=x_scales[:, q, cols],
                         start=(j == 0),
                         stop=(j == PASSES - 1),
                     )
@@ -142,9 +150,9 @@ def tile_morlet_coefficient_shrinkage_g1_kernel(tc, x, analysis, lam_sq, out_0, 
 
         def rsqrt(i):
             g = i // (2 * QUARTERS)
-            for tt in range(2):
-                t = 2 * (i % 2) + tt
-                cols = slice(tt * MW, (tt + 1) * MW)
+            ts, m0, mw = item(i)
+            for tt, t in enumerate(ts):
+                cols = slice(tt * mw, (tt + 1) * mw)
                 nc.scalar.activation(
                     out=r_t[:, i % RING, cols],
                     in_=e_t[:, i % RING, cols],
@@ -152,33 +160,34 @@ def tile_morlet_coefficient_shrinkage_g1_kernel(tc, x, analysis, lam_sq, out_0, 
                     bias=lam[:, g, t : t + 1],
                 )
 
-        def ratio(i):
+        def ratio(i, lo=0, hi=BANK):
             nc.vector.tensor_tensor(
-                out=u_t[:, i % RING, :], in0=c_bank[i % C_BANKS][:], in1=r_t[:, i % RING, :], op=MULT
+                out=u_t[:, i % RING, lo:hi], in0=c_bank[i % C_BANKS][:, lo:hi], in1=r_t[:, i % RING, lo:hi], op=MULT
             )
 
-        def gain(i):
-            nc.scalar.activation(out=g_t[:, i % RING, :], in_=u_t[:, i % RING, :], func=ACT.Square)
+        def gain(i, lo=0, hi=BANK):
+            nc.scalar.activation(out=g_t[:, i % RING, lo:hi], in_=u_t[:, i % RING, lo:hi], func=ACT.Square)
 
-        def shrink(i):
-            t = 2 * (i % 2)
+        def shrink(i, lo=0, hi=BANK):
+            ts, m0, mw = item(i)
             nc.vector.tensor_tensor(
-                out=y_t[:, i // 2, t : t + 2, :].rearrange("p t m -> p (t m)"),
-                in0=c_bank[i % C_BANKS][:],
-                in1=g_t[:, i % RING, :],
+                out=y_t[:, i // 2, ts[0] + lo // mw : ts[0] + hi // mw, m0 : m0 + mw],
+                in0=c_bank[i % C_BANKS][:, lo:hi].rearrange("p (t m) -> p t m", m=mw),
+                in1=g_t[:, i % RING, lo:hi].rearrange("p (t m) -> p t m", m=mw),
                 op=MULT,
             )
 
         def out_bank(block):
-            return t_bank[(M // P + block) % T_BANKS]
+            if block >= 28:
+                return c_bank[(block - 1) % C_BANKS]
+            return t_bank[block % T_BANKS]
 
-        def turn_y(unit):
-            for half in range(2):
-                bank = out_bank(2 * unit + half)
-                for t in range(PACK):
-                    nc.tensor.transpose(
-                        bank[:, t * P : (t + 1) * P], y_t[:, unit, t, half * P : (half + 1) * P], ident[:]
-                    )
+        def turn_y(block):
+            unit, half = divmod(block, 2)
+            for t in range(PACK):
+                nc.tensor.transpose(
+                    out_bank(block)[:, t * P : (t + 1) * P], y_t[:, unit, t, half * P : (half + 1) * P], ident[:]
+                )
 
         def store_y(engine, block):
             g, b = divmod(block, M // P)
@@ -199,6 +208,17 @@ def tile_morlet_coefficient_shrinkage_g1_kernel(tc, x, analysis, lam_sq, out_0, 
 
         def quant_y(u0, u1, stage):
             quantize(y_codes[:, u0 * MW : u1 * MW], y_scales[:, u0 * MW : u1 * MW], stage)
+
+        def round_block(engine, block, stage):
+            unit, half = divmod(block, 2)
+            copy(
+                engine,
+                stage.rearrange("p (m t) -> p m t", t=PACK),
+                y_t[:, unit, :, half * P : (half + 1) * P].rearrange("p t m -> p m t"),
+            )
+
+        def quant_block(block, stage):
+            quantize(y_codes[:, block * P : (block + 1) * P], y_scales[:, block * P : (block + 1) * P], stage)
 
         def store_words(u0, u1):
             for g in range(GROUPS):
@@ -221,52 +241,81 @@ def tile_morlet_coefficient_shrinkage_g1_kernel(tc, x, analysis, lam_sq, out_0, 
         lower, upper = g_stage[:, 0:W], g_stage[:, W : 2 * W]
         UW = MW * PACK
 
-        nc.vector.memset(warm[:, 0:1], 1.0)
-        nc.scalar.activation(out=warm[:, 8:9], in_=warm[:, 0:1], func=ACT.Abs_reciprocal_sqrt)
-        load_x(0, 1)
-        load_x(1, 2)
+        def load_lam():
+            with nc.allow_non_contiguous_dma(reason="four thresholds to a partition and group"):
+                nc.scalar.dma_start(out=lam[:], in_=lam_sq.rearrange("(g p t) -> p g t", p=P, t=PACK))
+
+        def warm_up():
+            nc.vector.memset(warm[:, 0:1], 1.0)
+            nc.scalar.activation(out=warm[:, 8:9], in_=warm[:, 0:1], func=ACT.Abs_reciprocal_sqrt)
+
+        def make_ident():
+            make_identity(nc, ident[:])
+
+        load_lam()
+        warm_up()
         load_a(0, 0)
         load_a(0, 1)
-        with nc.allow_non_contiguous_dma(reason="four thresholds to a partition and group"):
-            nc.scalar.dma_start(out=lam[:], in_=lam_sq.rearrange("(g p t) -> p g t", p=P, t=PACK))
-        for b in (2, 4, 6):
-            load_x(b, b + 2)
-        for g in range(1, GROUPS):
+        load_x(0, 1)
+        load_x(1, 2)
+        load_x(2, 4)
+        load_x(4, 6)
+        load_a(1, 0)
+        load_x(6, 8)
+        load_a(1, 1)
+        for g in range(2, GROUPS):
             for j in range(PASSES):
                 load_a(g, j)
-        make_identity(nc, ident[:])
+        make_ident()
 
-        turn_x(0)
-        turn_x(1)
-        copy_x("s", 0)
-        copy_x("s", 1)
-        turn_x(2)
-        turn_x(3)
-        weave_a("v", 0, 0, 0, 2, a_stage[:, 0, :])
-        weave_a("s", 0, 0, 2, 4, a_stage[:, 0, :])
-        weave_a("s", 0, 1, 2, 4, a_stage[:, 1, :])
-        quant_x(0)
-        quant_a(0, 0, 0, 2, a_stage[:, 0, :])
+        weave_a("v", 0, 0, 0, 4, a_stage[:, 0, :])
         weave_a("v", 0, 1, 0, 2, a_stage[:, 1, :])
-        quant_a(0, 0, 2, 4, a_stage[:, 0, :])
-        quant_a(0, 1, 0, 2, a_stage[:, 1, :])
+        weave_a("s", 0, 1, 2, 4, a_stage[:, 1, :])
+        quant_a(0, 0, 0, 4, a_stage[:, 0, :])
+        quant_a(0, 1, 0, 4, a_stage[:, 1, :])
+        for b in range(6):
+            turn_x(b)
+            copy_x("v" if b in (1, 3) else "s", b)
+            if b in (1, 3):
+                quant_x(b // 2)
         multiply(0)
-        copy_x("v", 2)
-        quant_a(0, 1, 2, 4, a_stage[:, 1, :])
         multiply(1)
-        copy_x("v", 3)
-        quant_x(1)
+        weave_a("v", 1, 0, 0, 4, a_stage[:, 0, :])
+        quant_x(2)
+        turn_x(6)
+        turn_x(7)
+        square_c(0)
+        square_c(1)
+        rsqrt(0)
+        rsqrt(1)
+        copy_x("s", 6)
+        copy_x("v", 7)
+        quant_a(1, 0, 0, 4, a_stage[:, 0, :])
+        quant_x(3)
+        weave_a("g", 1, 1, 0, 4, lower)
+        weave_a("g", 2, 0, 0, 4, upper)
+        for i in (2, 3, 4):
+            multiply(i)
+        square_c(2)
+        square_c(3)
+        rsqrt(2)
+        square_c(4)
+        for i in range(3):
+            ratio(i)
+        gain(0)
+        rsqrt(3)
+        gain(1)
+        gain(2)
+        shrink(0)
+        multiply(5)
+        shrink(1)
+        multiply(6)
+        ratio(3)
 
         def slot(s):
-            if s == 2:
-                quant_x(2)
-            elif s == 3:
-                quant_x(3)
-                weave_a("g", 1, 1, 0, 4, lower)
-                weave_a("g", 2, 0, 0, 4, upper)
-            elif s == 7:
-                quant_a(1, 0, 0, 4, a_stage[:, 2, :])
+            if s == 7:
                 quant_a(1, 1, 0, 4, lower)
+                multiply(8)
                 quant_a(2, 0, 0, 4, upper)
                 weave_a("g", 2, 1, 0, 4, upper)
                 round_y("g", 0, 1, lower[:, 0:UW])
@@ -287,73 +336,72 @@ def tile_morlet_coefficient_shrinkage_g1_kernel(tc, x, analysis, lam_sq, out_0, 
                 quant_y(2, 3, lower[:, 0:UW])
                 store_words(2, 3)
                 round_y("g", 3, 6, g_stage[:, 0 : 3 * UW])
-            elif s in (23, 27, 31):
+            elif s in (23, 27):
                 u0 = 3 + 3 * ((s - 23) // 4)
                 quant_y(u0, u0 + 2, g_stage[:, 0 : 2 * UW])
                 quant_y(u0 + 2, u0 + 3, g_stage[:, 2 * UW : 3 * UW])
                 store_words(u0, u0 + 3)
-                u1 = min(u0 + 6, UNITS - 2)
-                round_y("g", u0 + 3, u1, g_stage[:, 0 : (u1 - u0 - 3) * UW])
-                if s == 31:
-                    store_scales(0, 3)
+                round_y("g", u0 + 3, u0 + 6, g_stage[:, 0 : 3 * UW])
 
-        for s in range(ITEMS + 3):
+        ON_SCALAR = (7, 11, 19, 23, 27)
+        for s in range(5, 30):
             slot(s)
-            if s == 0:
-                turn_x(4)
-                turn_x(5)
-            if s == 1:
-                turn_x(6)
-                turn_x(7)
-            if s >= 5 and s % 2 == 1:
-                turn_y((s - 5) // 2)
+            if s % 2 == 1:
+                turn_y(s - 5)
+                turn_y(s - 4)
             block = s - 6
-            if s == 2:
-                copy_x("v", 7)
-            if s == 0:
-                copy_x("v", 4)
-                copy_x("v", 5)
-            if 0 <= block and s % 8 != 3 and s < ITEMS:
+            if 0 <= block and s not in ON_SCALAR:
                 store_y("v", block)
-            if 1 <= s <= ITEMS:
-                rsqrt(s - 1)
-            if s < ITEMS:
-                square_c(s)
-            if 2 <= s <= ITEMS + 1:
-                gain(s - 2)
-            if s == 2:
-                weave_a("s", 1, 0, 0, 2, a_stage[:, 2, :])
-            if s == 4:
-                weave_a("s", 1, 0, 2, 4, a_stage[:, 2, :])
-            if 0 <= block and s % 8 == 3 and s < ITEMS:
+            rsqrt(s - 1)
+            square_c(s)
+            gain(s - 2)
+            if 0 <= block and s in ON_SCALAR:
                 store_y("s", block)
-            if s == ITEMS:
-                store_y("s", 26)
-                store_y("s", 27)
-            if s == ITEMS + 1:
-                store_y("s", 28)
-                store_y("s", 29)
-            if s == ITEMS + 2:
-                round_y("s", 14, 15, tail_stage[:, 0:UW])
-            if s == ITEMS + 1:
-                quant_y(12, 14, g_stage[:, 0 : 2 * UW])
-                store_words(12, 14)
-            if s >= 3:
-                shrink(s - 3)
-            if 1 <= s <= ITEMS:
-                ratio(s - 1)
-            if s == 1:
-                copy_x("v", 6)
-            if s == 7:
-                multiply(8)
+            shrink(s - 3)
+            ratio(s - 1)
             if s + 2 < ITEMS and s != 6:
                 multiply(s + 2)
 
-        turn_y(UNITS - 1)
-        quant_y(14, 15, tail_stage[:, 0:UW])
-        round_y("v", 15, 16, tail_stage[:, UW : 2 * UW])
+        store_y("v", 24)
+        rsqrt(29)
+        square_c(30)
+        gain(28)
+        shrink(27)
+        quant_y(11, 12, g_stage[:, 2 * UW : 3 * UW])
+        quant_y(9, 11, g_stage[:, 0 : 2 * UW])
+        round_y("g", 12, 14, g_stage[:, 0 : 2 * UW])
+        ratio(29)
+        turn_y(26)
+        store_y("v", 25)
+        store_words(9, 12)
+        store_scales(0, 3)
+        turn_y(27)
+        rsqrt(30)
+        square_c(31)
+        gain(29)
+        rsqrt(31)
+        shrink(28)
+        ratio(30)
+        shrink(29)
+        round_y("g", 14, 15, g_stage[:, 2 * UW : 3 * UW])
+        turn_y(28)
+        turn_y(29)
+        store_y("s", 26)
+        gain(30)
+        ratio(31)
+        store_y("v", 27)
+        gain(31)
+        shrink(30)
+        turn_y(30)
+        shrink(31)
+        turn_y(31)
+        store_y("s", 28)
+        store_y("s", 29)
+        quant_y(12, 14, g_stage[:, 0 : 2 * UW])
+        store_words(12, 14)
+        round_y("v", 15, 16, g_stage[:, 3 * UW : 4 * UW])
         store_y("s", 30)
         store_y("s", 31)
-        quant_y(15, 16, tail_stage[:, UW : 2 * UW])
-        store_words(14, 16)
+        quant_y(14, 16, g_stage[:, 2 * UW : 4 * UW])
         store_scales(3, 4)
+        store_words(14, 16)

@@ -62,7 +62,7 @@ def tile_morlet_coefficient_shrinkage_g1_kernel(tc, x, analysis, lam_sq, out_0, 
         r_t = sb.tile([P, RING, BANK], F32, name="r_t")
         u_t = sb.tile([P, RING, BANK], F32, name="u_t")
         g_t = sb.tile([P, RING, BANK], F32, name="g_t")
-        y_t = sb.tile([P, UNITS, PACK, MW], F32, name="y_t")
+        y_t = sb.tile([P, PACK, UNITS * MW], F32, name="y_t")
         o_t = sb.tile([P, OUT_RING, BANK], F32, name="o_t")
         c_bank = [ps.tile([P, BANK], F32, name="c_bank%d" % b) for b in range(C_BANKS)]
         t_bank = [ps.tile([P, BANK], F32, name="t_bank%d" % b) for b in range(T_BANKS)]
@@ -171,7 +171,7 @@ def tile_morlet_coefficient_shrinkage_g1_kernel(tc, x, analysis, lam_sq, out_0, 
         def shrink(i, lo=0, hi=BANK):
             ts, m0, mw = item(i)
             nc.vector.tensor_tensor(
-                out=y_t[:, i // 2, ts[0] + lo // mw : ts[0] + hi // mw, m0 : m0 + mw],
+                out=y_t[:, ts[0] + lo // mw : ts[0] + hi // mw, i // 2 * MW + m0 : i // 2 * MW + m0 + mw],
                 in0=c_bank[i % C_BANKS][:, lo:hi].rearrange("p (t m) -> p t m", m=mw),
                 in1=g_t[:, i % RING, lo:hi].rearrange("p (t m) -> p t m", m=mw),
                 op=MULT,
@@ -186,7 +186,7 @@ def tile_morlet_coefficient_shrinkage_g1_kernel(tc, x, analysis, lam_sq, out_0, 
             unit, half = divmod(block, 2)
             for t in range(PACK):
                 nc.tensor.transpose(
-                    out_bank(block)[:, t * P : (t + 1) * P], y_t[:, unit, t, half * P : (half + 1) * P], ident[:]
+                    out_bank(block)[:, t * P : (t + 1) * P], y_t[:, t, block * P : (block + 1) * P], ident[:]
                 )
 
         def store_y(engine, block):
@@ -202,23 +202,12 @@ def tile_morlet_coefficient_shrinkage_g1_kernel(tc, x, analysis, lam_sq, out_0, 
         def round_y(engine, u0, u1, stage):
             copy(
                 engine,
-                stage.rearrange("p (u m t) -> p u m t", m=MW, t=PACK),
-                y_t[:, u0:u1].rearrange("p u t m -> p u m t"),
+                stage.rearrange("p (c i t) -> p c t i", i=4, t=PACK),
+                y_t[:, :, u0 * MW : u1 * MW].rearrange("p t (c i) -> p c t i", i=4),
             )
 
         def quant_y(u0, u1, stage):
             quantize(y_codes[:, u0 * MW : u1 * MW], y_scales[:, u0 * MW : u1 * MW], stage)
-
-        def round_block(engine, block, stage):
-            unit, half = divmod(block, 2)
-            copy(
-                engine,
-                stage.rearrange("p (m t) -> p m t", t=PACK),
-                y_t[:, unit, :, half * P : (half + 1) * P].rearrange("p t m -> p m t"),
-            )
-
-        def quant_block(block, stage):
-            quantize(y_codes[:, block * P : (block + 1) * P], y_scales[:, block * P : (block + 1) * P], stage)
 
         def store_words(u0, u1):
             for g in range(GROUPS):

@@ -21,11 +21,15 @@ K_PASS = P * PACK
 PASSES = K // K_PASS
 GROUP = P * PACK
 GROUPS = N // GROUP
-MW = 256
-QUARTERS = M // MW
+UNIT_M = 256
+QUARTERS = M // UNIT_M
 UNITS = GROUPS * QUARTERS
 ITEMS = 2 * UNITS
+X_TILES = M // P
 BANK = 512
+PASS_COLS = GROUP * PACK
+UNIT_COLS = UNIT_M * PACK
+
 C_BANKS = 5
 T_BANKS = 3
 RING = 4
@@ -34,8 +38,8 @@ OUT_RING = 8
 
 def tile_morlet_coefficient_shrinkage_g1_kernel(tc, x, analysis, lam_sq, out_0, out_1, out_2):
     nc = tc.nc
-    x2 = x.rearrange("a b k -> (a b) k")
-    y2 = out_0.rearrange("a b n -> (a b) n")
+    x_rows = x.rearrange("a b k -> (a b) k")
+    y_rows = out_0.rearrange("a b n -> (a b) n")
     words_hbm = out_1.rearrange("g p m t -> g p (m t)").bitcast(I32)
     scales_hbm = out_2.bitcast(I32)
 
@@ -47,13 +51,13 @@ def tile_morlet_coefficient_shrinkage_g1_kernel(tc, x, analysis, lam_sq, out_0, 
         ident = sb.tile([P, P], F32, name="ident")
         warm = sb.tile([P, 16], F32, name="warm")
         lam = sb.tile([P, GROUPS, PACK], BF16, name="lam")
-        x_raw = sb.tile([P, M // P, K], BF16, name="x_raw")
+        x_raw = sb.tile([P, X_TILES, K], BF16, name="x_raw")
         a_raw = sb.tile([P, GROUPS, PASSES, PACK, GROUP], BF16, name="a_raw")
-        x_stage = sb.tile([P, QUARTERS - 1, PASSES * MW * PACK], BF16, name="x_stage", align_bytes=64)
-        a_stage = sb.tile([P, 2, GROUP * PACK], BF16, name="a_stage", align_bytes=64)
-        g_stage = sb.tile([P, 2 * GROUP * PACK], BF16, name="g_stage", align_bytes=64)
-        x_codes = sb.tile([P, QUARTERS, PASSES * MW], U32, name="x_codes", align_bytes=64)
-        x_scales = sb.tile([P, QUARTERS, PASSES * MW], U8, name="x_scales", align_bytes=64)
+        x_stage = sb.tile([P, QUARTERS - 1, PASSES * UNIT_COLS], BF16, name="x_stage", align_bytes=64)
+        a_stage = sb.tile([P, 2, PASS_COLS], BF16, name="a_stage", align_bytes=64)
+        g_stage = sb.tile([P, 2 * PASS_COLS], BF16, name="g_stage", align_bytes=64)
+        x_codes = sb.tile([P, QUARTERS, PASSES * UNIT_M], U32, name="x_codes", align_bytes=64)
+        x_scales = sb.tile([P, QUARTERS, PASSES * UNIT_M], U8, name="x_scales", align_bytes=64)
         a_codes = sb.tile([P, GROUPS, PASSES, GROUP], U32, name="a_codes", align_bytes=64)
         a_scales = sb.tile([P, GROUPS, PASSES, GROUP], U8, name="a_scales", align_bytes=64)
         y_codes = sb.tile([P, GROUPS * M], U32, name="y_codes", align_bytes=64)
@@ -62,81 +66,87 @@ def tile_morlet_coefficient_shrinkage_g1_kernel(tc, x, analysis, lam_sq, out_0, 
         r_t = sb.tile([P, RING, BANK], F32, name="r_t")
         u_t = sb.tile([P, RING, BANK], F32, name="u_t")
         g_t = sb.tile([P, RING, BANK], F32, name="g_t")
-        y_t = sb.tile([P, PACK, UNITS * MW], F32, name="y_t")
+        y_t = sb.tile([P, UNITS, PACK, UNIT_M], F32, name="y_t")
         o_t = sb.tile([P, OUT_RING, BANK], F32, name="o_t")
         c_bank = [ps.tile([P, BANK], F32, name="c_bank%d" % b) for b in range(C_BANKS)]
         t_bank = [ps.tile([P, BANK], F32, name="t_bank%d" % b) for b in range(T_BANKS)]
 
+        lower, upper = g_stage[:, 0:PASS_COLS], g_stage[:, PASS_COLS : 2 * PASS_COLS]
+
+        def g_units(first, last):
+            return g_stage[:, first * UNIT_COLS : last * UNIT_COLS]
+
         def copy(engine, out, in_):
-            if engine == "s":
+            if engine == "scalar":
                 nc.scalar.copy(out=out, in_=in_)
-            elif engine == "v":
+            elif engine == "vector":
                 nc.vector.tensor_copy(out=out, in_=in_)
             else:
                 nc.gpsimd.tensor_scalar(out=out, in0=in_, scalar1=1.0, scalar2=1.0, op0=MULT, op1=MULT)
 
-        def load_x(b0, b1):
-            nc.sync.dma_start(
-                out=x_raw[:, b0:b1, :], in_=x2[b0 * P : b1 * P, :].rearrange("(b p) k -> p b k", p=P)
-            )
+        def quantize(codes, scales, src):
+            nc.vector.quantize_mx(out=codes.bitcast(FP8X4), scales=scales, in_=src)
 
-        def load_a(g, j):
-            rows = analysis[j * K_PASS : (j + 1) * K_PASS, g * GROUP : (g + 1) * GROUP]
-            nc.sync.dma_start(out=a_raw[:, g, j, :, :], in_=rows.rearrange("(p r) n -> p r n", r=PACK))
+
+        def load_x(first, last):
+            rows = x_rows[first * P : last * P, :]
+            nc.sync.dma_start(out=x_raw[:, first:last, :], in_=rows.rearrange("(b p) k -> p b k", p=P))
 
         def x_stage_of(q):
-            return g_stage[:, 0 : GROUP * PACK] if q == 3 else x_stage[:, q, :]
+            return lower if q == QUARTERS - 1 else x_stage[:, q, :]
 
         def x_bank(b):
             return (t_bank + [c_bank[4], c_bank[3]] + t_bank)[b]
 
         def turn_x(b):
             words = x_raw[:, b, :].bitcast(F32)
-            bank = x_bank(b)
+            half = K_PASS // 2
             for j in range(PASSES):
                 for h in range(2):
                     col = (2 * j + h) * P
                     nc.tensor.transpose(
-                        bank[:, col : col + P], words[:, 256 * j + h : 256 * (j + 1) : 2], ident[:]
+                        x_bank(b)[:, col : col + P], words[:, half * j + h : half * (j + 1) : 2], ident[:]
                     )
 
         def copy_x(engine, b):
             dst = x_stage_of(b // 2).bitcast(F32).rearrange("p (j m h) -> p j m h", j=PASSES, h=2)
-            half = b % 2
+            m0 = (b % 2) * P
             copy(
                 engine,
-                dst[:, :, half * P : (half + 1) * P, :],
+                dst[:, :, m0 : m0 + P, :],
                 x_bank(b)[:].rearrange("p (j h m) -> p j m h", j=PASSES, h=2),
             )
-
-        def quantize(codes, scales, src):
-            nc.vector.quantize_mx(out=codes.bitcast(FP8X4), scales=scales, in_=src)
 
         def quant_x(q):
             quantize(x_codes[:, q, :], x_scales[:, q, :], x_stage_of(q))
 
-        def weave_a(engine, g, j, t0, t1, stage):
+
+        def load_a(g, j):
+            rows = analysis[j * K_PASS : (j + 1) * K_PASS, g * GROUP : (g + 1) * GROUP]
+            nc.sync.dma_start(out=a_raw[:, g, j, :, :], in_=rows.rearrange("(p r) n -> p r n", r=PACK))
+
+        def weave_a(engine, g, j, stage, t0=0, t1=PACK):
             src = a_raw[:, g, j, :, :].rearrange("p r (c t) -> p t c r", t=PACK)
             dst = stage.rearrange("p (t c r) -> p t c r", t=PACK, r=PACK)
             copy(engine, dst[:, t0:t1], src[:, t0:t1])
 
-        def quant_a(g, j, t0, t1, stage):
-            cols = slice(t0 * P, t1 * P)
-            quantize(a_codes[:, g, j, cols], a_scales[:, g, j, cols], stage[:, t0 * GROUP : t1 * GROUP])
+        def quant_a(g, j, stage):
+            quantize(a_codes[:, g, j, :], a_scales[:, g, j, :], stage)
+
 
         def item(i):
             if i // 2 < UNITS - 1:
-                return range(2 * (i % 2), 2 * (i % 2) + 2), 0, MW
+                return range(2 * (i % 2), 2 * (i % 2) + 2), 0, UNIT_M
             return range(PACK), (i % 2) * P, P
 
         def multiply(i):
             g, q = divmod(i // 2, QUARTERS)
-            ts, m0, mw = item(i)
-            for tt, t in enumerate(ts):
+            slices, m0, width = item(i)
+            for place, t in enumerate(slices):
                 for j in range(PASSES):
-                    cols = slice(j * MW + m0, j * MW + m0 + mw)
+                    cols = slice(j * UNIT_M + m0, j * UNIT_M + m0 + width)
                     nc.tensor.matmul_mx(
-                        out=c_bank[i % C_BANKS][:, tt * mw : (tt + 1) * mw],
+                        out=c_bank[i % C_BANKS][:, place * width : (place + 1) * width],
                         lhsT=a_codes[:, g, j, t * P : (t + 1) * P].bitcast(FP8X4),
                         lhsT_scale=a_scales[:, g, j, t * P : (t + 1) * P],
                         rhs=x_codes[:, q, cols].bitcast(FP8X4),
@@ -150,9 +160,9 @@ def tile_morlet_coefficient_shrinkage_g1_kernel(tc, x, analysis, lam_sq, out_0, 
 
         def rsqrt(i):
             g = i // (2 * QUARTERS)
-            ts, m0, mw = item(i)
-            for tt, t in enumerate(ts):
-                cols = slice(tt * mw, (tt + 1) * mw)
+            slices, m0, width = item(i)
+            for place, t in enumerate(slices):
+                cols = slice(place * width, (place + 1) * width)
                 nc.scalar.activation(
                     out=r_t[:, i % RING, cols],
                     in_=e_t[:, i % RING, cols],
@@ -160,25 +170,26 @@ def tile_morlet_coefficient_shrinkage_g1_kernel(tc, x, analysis, lam_sq, out_0, 
                     bias=lam[:, g, t : t + 1],
                 )
 
-        def ratio(i, lo=0, hi=BANK):
+        def ratio(i):
             nc.vector.tensor_tensor(
-                out=u_t[:, i % RING, lo:hi], in0=c_bank[i % C_BANKS][:, lo:hi], in1=r_t[:, i % RING, lo:hi], op=MULT
+                out=u_t[:, i % RING, :], in0=c_bank[i % C_BANKS][:], in1=r_t[:, i % RING, :], op=MULT
             )
 
-        def gain(i, lo=0, hi=BANK):
-            nc.scalar.activation(out=g_t[:, i % RING, lo:hi], in_=u_t[:, i % RING, lo:hi], func=ACT.Square)
+        def gain(i):
+            nc.scalar.activation(out=g_t[:, i % RING, :], in_=u_t[:, i % RING, :], func=ACT.Square)
 
-        def shrink(i, lo=0, hi=BANK):
-            ts, m0, mw = item(i)
+        def shrink(i):
+            slices, m0, width = item(i)
             nc.vector.tensor_tensor(
-                out=y_t[:, ts[0] + lo // mw : ts[0] + hi // mw, i // 2 * MW + m0 : i // 2 * MW + m0 + mw],
-                in0=c_bank[i % C_BANKS][:, lo:hi].rearrange("p (t m) -> p t m", m=mw),
-                in1=g_t[:, i % RING, lo:hi].rearrange("p (t m) -> p t m", m=mw),
+                out=y_t[:, i // 2, slices[0] : slices[-1] + 1, m0 : m0 + width],
+                in0=c_bank[i % C_BANKS][:].rearrange("p (t m) -> p t m", m=width),
+                in1=g_t[:, i % RING, :].rearrange("p (t m) -> p t m", m=width),
                 op=MULT,
             )
 
+
         def out_bank(block):
-            if block >= 28:
+            if block >= ITEMS - 4:
                 return c_bank[(block - 1) % C_BANKS]
             return t_bank[block % T_BANKS]
 
@@ -186,63 +197,52 @@ def tile_morlet_coefficient_shrinkage_g1_kernel(tc, x, analysis, lam_sq, out_0, 
             unit, half = divmod(block, 2)
             for t in range(PACK):
                 nc.tensor.transpose(
-                    out_bank(block)[:, t * P : (t + 1) * P], y_t[:, t, block * P : (block + 1) * P], ident[:]
+                    out_bank(block)[:, t * P : (t + 1) * P], y_t[:, unit, t, half * P : (half + 1) * P], ident[:]
                 )
 
         def store_y(engine, block):
-            g, b = divmod(block, M // P)
+            g, b = divmod(block, X_TILES)
             dst = o_t[:, block % OUT_RING, :]
             copy(
                 engine,
                 dst.rearrange("m (p t) -> m p t", t=PACK),
                 out_bank(block)[:].rearrange("m (t p) -> m p t", t=PACK),
             )
-            nc.sync.dma_start(out=y2[b * P : (b + 1) * P, g * GROUP : (g + 1) * GROUP], in_=dst)
+            nc.sync.dma_start(out=y_rows[b * P : (b + 1) * P, g * GROUP : (g + 1) * GROUP], in_=dst)
 
-        def round_y(engine, u0, u1, stage):
+
+        def round_y(engine, first, last, stage):
             copy(
                 engine,
-                stage.rearrange("p (c i t) -> p c t i", i=4, t=PACK),
-                y_t[:, :, u0 * MW : u1 * MW].rearrange("p t (c i) -> p c t i", i=4),
+                stage.rearrange("p (u m t) -> p u m t", m=UNIT_M, t=PACK),
+                y_t[:, first:last].rearrange("p u t m -> p u m t"),
             )
 
-        def quant_y(u0, u1, stage):
-            quantize(y_codes[:, u0 * MW : u1 * MW], y_scales[:, u0 * MW : u1 * MW], stage)
+        def quant_y(first, last, stage):
+            cols = slice(first * UNIT_M, last * UNIT_M)
+            quantize(y_codes[:, cols], y_scales[:, cols], stage)
 
-        def store_words(u0, u1):
-            for g in range(GROUPS):
-                lo, hi = max(u0, g * QUARTERS), min(u1, (g + 1) * QUARTERS)
-                if lo < hi:
-                    nc.sync.dma_start(
-                        out=words_hbm[g, :, (lo - g * QUARTERS) * MW : (hi - g * QUARTERS) * MW],
-                        in_=y_codes[:, lo * MW : hi * MW].bitcast(I32),
-                    )
+        def store_words(first, last):
+            for g in range(first // QUARTERS, (last - 1) // QUARTERS + 1):
+                lo, hi = max(first, g * QUARTERS), min(last, (g + 1) * QUARTERS)
+                nc.sync.dma_start(
+                    out=words_hbm[g, :, (lo - g * QUARTERS) * UNIT_M : (hi - g * QUARTERS) * UNIT_M],
+                    in_=y_codes[:, lo * UNIT_M : hi * UNIT_M].bitcast(I32),
+                )
 
-        def store_scales(g0, g1):
+        def store_scales(first, last):
             plane = y_scales[:].bitcast(I32).rearrange("p (g w) -> p g w", g=GROUPS)
             for quad in range(4):
                 nc.sync.dma_start(
-                    out=scales_hbm[g0:g1, 4 * quad : 4 * quad + 4, :].rearrange("g r w -> r g w"),
-                    in_=plane[32 * quad : 32 * quad + 4, g0:g1, :],
+                    out=scales_hbm[first:last, 4 * quad : 4 * quad + 4, :].rearrange("g r w -> r g w"),
+                    in_=plane[32 * quad : 32 * quad + 4, first:last, :],
                 )
 
-        W = GROUP * PACK
-        lower, upper = g_stage[:, 0:W], g_stage[:, W : 2 * W]
-        UW = MW * PACK
 
-        def load_lam():
-            with nc.allow_non_contiguous_dma(reason="four thresholds to a partition and group"):
-                nc.scalar.dma_start(out=lam[:], in_=lam_sq.rearrange("(g p t) -> p g t", p=P, t=PACK))
-
-        def warm_up():
-            nc.vector.memset(warm[:, 0:1], 1.0)
-            nc.scalar.activation(out=warm[:, 8:9], in_=warm[:, 0:1], func=ACT.Abs_reciprocal_sqrt)
-
-        def make_ident():
-            make_identity(nc, ident[:])
-
-        load_lam()
-        warm_up()
+        with nc.allow_non_contiguous_dma(reason="four thresholds to a partition and group"):
+            nc.scalar.dma_start(out=lam[:], in_=lam_sq.rearrange("(g p t) -> p g t", p=P, t=PACK))
+        nc.vector.memset(warm[:, 0:1], 1.0)
+        nc.scalar.activation(out=warm[:, 8:9], in_=warm[:, 0:1], func=ACT.Abs_reciprocal_sqrt)
         load_a(0, 0)
         load_a(0, 1)
         load_x(0, 1)
@@ -255,21 +255,21 @@ def tile_morlet_coefficient_shrinkage_g1_kernel(tc, x, analysis, lam_sq, out_0, 
         for g in range(2, GROUPS):
             for j in range(PASSES):
                 load_a(g, j)
-        make_ident()
+        make_identity(nc, ident[:])
 
-        weave_a("v", 0, 0, 0, 4, a_stage[:, 0, :])
-        weave_a("v", 0, 1, 0, 2, a_stage[:, 1, :])
-        weave_a("s", 0, 1, 2, 4, a_stage[:, 1, :])
-        quant_a(0, 0, 0, 4, a_stage[:, 0, :])
-        quant_a(0, 1, 0, 4, a_stage[:, 1, :])
+        weave_a("vector", 0, 0, a_stage[:, 0, :])
+        weave_a("vector", 0, 1, a_stage[:, 1, :], 0, 2)
+        weave_a("scalar", 0, 1, a_stage[:, 1, :], 2, 4)
+        quant_a(0, 0, a_stage[:, 0, :])
+        quant_a(0, 1, a_stage[:, 1, :])
         for b in range(6):
             turn_x(b)
-            copy_x("v" if b in (1, 3) else "s", b)
+            copy_x("scalar", b)
             if b in (1, 3):
                 quant_x(b // 2)
         multiply(0)
         multiply(1)
-        weave_a("v", 1, 0, 0, 4, a_stage[:, 0, :])
+        weave_a("vector", 1, 0, a_stage[:, 0, :])
         quant_x(2)
         turn_x(6)
         turn_x(7)
@@ -277,12 +277,13 @@ def tile_morlet_coefficient_shrinkage_g1_kernel(tc, x, analysis, lam_sq, out_0, 
         square_c(1)
         rsqrt(0)
         rsqrt(1)
-        copy_x("s", 6)
-        copy_x("v", 7)
-        quant_a(1, 0, 0, 4, a_stage[:, 0, :])
+        copy_x("scalar", 6)
+        copy_x("vector", 7)
+        quant_a(1, 0, a_stage[:, 0, :])
         quant_x(3)
-        weave_a("g", 1, 1, 0, 4, lower)
-        weave_a("g", 2, 0, 0, 4, upper)
+        weave_a("gpsimd", 1, 1, lower)
+        weave_a("gpsimd", 2, 0, upper)
+
         for i in (2, 3, 4):
             multiply(i)
         square_c(2)
@@ -301,67 +302,72 @@ def tile_morlet_coefficient_shrinkage_g1_kernel(tc, x, analysis, lam_sq, out_0, 
         multiply(6)
         ratio(3)
 
-        def slot(s):
-            if s == 7:
-                quant_a(1, 1, 0, 4, lower)
-                multiply(8)
-                quant_a(2, 0, 0, 4, upper)
-                weave_a("g", 2, 1, 0, 4, upper)
-                round_y("g", 0, 1, lower[:, 0:UW])
-            elif s == 11:
-                quant_a(2, 1, 0, 4, upper)
-                quant_y(0, 1, lower[:, 0:UW])
-                store_words(0, 1)
-                weave_a("g", 3, 0, 0, 4, lower)
-                round_y("g", 1, 2, upper[:, 0:UW])
-            elif s == 15:
-                quant_a(3, 0, 0, 4, lower)
-                quant_y(1, 2, upper[:, 0:UW])
-                store_words(1, 2)
-                weave_a("g", 3, 1, 0, 4, upper)
-                round_y("g", 2, 3, lower[:, 0:UW])
-            elif s == 19:
-                quant_a(3, 1, 0, 4, upper)
-                quant_y(2, 3, lower[:, 0:UW])
-                store_words(2, 3)
-                round_y("g", 3, 6, g_stage[:, 0 : 3 * UW])
-            elif s in (23, 27):
-                u0 = 3 + 3 * ((s - 23) // 4)
-                quant_y(u0, u0 + 2, g_stage[:, 0 : 2 * UW])
-                quant_y(u0 + 2, u0 + 3, g_stage[:, 2 * UW : 3 * UW])
-                store_words(u0, u0 + 3)
-                round_y("g", u0 + 3, u0 + 6, g_stage[:, 0 : 3 * UW])
+        first_step, last_step = 5, ITEMS - 3
+        first_hand_over, period = 7, 4
 
-        ON_SCALAR = (7, 11, 19, 23, 27)
-        for s in range(5, 30):
-            slot(s)
+        def hand_over(n):
+            if n == 0:
+                quant_a(1, 1, lower)
+                multiply(8)
+                quant_a(2, 0, upper)
+                weave_a("gpsimd", 2, 1, upper)
+                round_y("gpsimd", 0, 1, g_units(0, 1))
+            elif n == 1:
+                quant_a(2, 1, upper)
+                quant_y(0, 1, g_units(0, 1))
+                store_words(0, 1)
+                weave_a("gpsimd", 3, 0, lower)
+                round_y("gpsimd", 1, 2, g_units(2, 3))
+            elif n == 2:
+                quant_a(3, 0, lower)
+                quant_y(1, 2, g_units(2, 3))
+                store_words(1, 2)
+                weave_a("gpsimd", 3, 1, upper)
+                round_y("gpsimd", 2, 3, g_units(0, 1))
+            elif n == 3:
+                quant_a(3, 1, upper)
+                quant_y(2, 3, g_units(0, 1))
+                store_words(2, 3)
+                round_y("gpsimd", 3, 6, g_units(0, 3))
+            else:
+                staged = 3 * (n - 3)
+                quant_y(staged, staged + 2, g_units(0, 2))
+                quant_y(staged + 2, staged + 3, g_units(2, 3))
+                store_words(staged, staged + 3)
+                round_y("gpsimd", staged + 3, staged + 6, g_units(0, 3))
+
+        for s in range(first_step, last_step + 1):
+            n, phase = divmod(s - first_hand_over, period)
+            vector_quantises = n >= 0 and phase == 0
+            if vector_quantises:
+                hand_over(n)
             if s % 2 == 1:
                 turn_y(s - 5)
                 turn_y(s - 4)
             block = s - 6
-            if 0 <= block and s not in ON_SCALAR:
-                store_y("v", block)
+            if block >= 0 and not vector_quantises:
+                store_y("vector", block)
             rsqrt(s - 1)
             square_c(s)
             gain(s - 2)
-            if 0 <= block and s in ON_SCALAR:
-                store_y("s", block)
+            if vector_quantises:
+                store_y("scalar", block)
             shrink(s - 3)
             ratio(s - 1)
-            if s + 2 < ITEMS and s != 6:
+            if s != first_hand_over - 1:
                 multiply(s + 2)
 
-        store_y("v", 24)
+        store_y("vector", 24)
         rsqrt(29)
         square_c(30)
         gain(28)
         shrink(27)
-        quant_y(11, 12, g_stage[:, 2 * UW : 3 * UW])
-        quant_y(9, 11, g_stage[:, 0 : 2 * UW])
-        round_y("g", 12, 14, g_stage[:, 0 : 2 * UW])
+        quant_y(11, 12, g_units(2, 3))
+        quant_y(9, 11, g_units(0, 2))
+        round_y("gpsimd", 12, 14, g_units(0, 2))
         ratio(29)
         turn_y(26)
-        store_y("v", 25)
+        store_y("scalar", 25)
         store_words(9, 12)
         store_scales(0, 3)
         turn_y(27)
@@ -372,25 +378,25 @@ def tile_morlet_coefficient_shrinkage_g1_kernel(tc, x, analysis, lam_sq, out_0, 
         shrink(28)
         ratio(30)
         shrink(29)
-        round_y("g", 14, 15, g_stage[:, 2 * UW : 3 * UW])
+        round_y("gpsimd", 14, 15, g_units(2, 3))
         turn_y(28)
         turn_y(29)
-        store_y("s", 26)
+        store_y("scalar", 26)
         gain(30)
         ratio(31)
-        store_y("v", 27)
+        store_y("vector", 27)
         gain(31)
         shrink(30)
         turn_y(30)
         shrink(31)
         turn_y(31)
-        store_y("s", 28)
-        store_y("s", 29)
-        quant_y(12, 14, g_stage[:, 0 : 2 * UW])
+        store_y("scalar", 28)
+        store_y("scalar", 29)
+        quant_y(12, 14, g_units(0, 2))
         store_words(12, 14)
-        round_y("v", 15, 16, g_stage[:, 3 * UW : 4 * UW])
-        store_y("s", 30)
-        store_y("s", 31)
-        quant_y(14, 16, g_stage[:, 2 * UW : 4 * UW])
+        round_y("scalar", 15, 16, g_units(3, 4))
+        store_y("vector", 30)
+        store_y("vector", 31)
+        quant_y(14, 16, g_units(2, 4))
         store_scales(3, 4)
         store_words(14, 16)

from contextlib import ExitStack

import concourse.mybir as mybir
from concourse.masks import make_identity

M, K, N = 1024, 1024, 2048
FLOPS = 2 * M * K * N

F32 = mybir.dt.float32
BF16 = mybir.dt.bfloat16
I32 = mybir.dt.int32
U32 = mybir.dt.uint32
U8 = mybir.dt.uint8
FP8X4 = mybir.dt.float8_e4m3fn_x4
ACT = mybir.ActivationFunctionType
MULT = mybir.AluOpType.mult

P = 128
PACK = 4
K_PASS = P * PACK
PASSES = K // K_PASS
GROUP = P * PACK
GROUPS = N // GROUP
UNIT_M = 256
QUARTERS = M // UNIT_M
UNITS = GROUPS * QUARTERS
ITEMS = 2 * UNITS
X_TILES = M // P
BANK = 512
PASS_COLS = GROUP * PACK
UNIT_COLS = UNIT_M * PACK

C_BANKS = 5
T_BANKS = 3
RING = 4
OUT_RING = 8


def tile_morlet_coefficient_shrinkage_g1_kernel(tc, x, analysis, lam_sq, out_0, out_1, out_2):
    nc = tc.nc
    x_rows = x.rearrange("a b k -> (a b) k")
    y_rows = out_0.rearrange("a b n -> (a b) n")
    words_hbm = out_1.rearrange("g p m t -> g p (m t)").bitcast(I32)
    scales_hbm = out_2.bitcast(I32)

    with ExitStack() as ctx:
        sb = ctx.enter_context(tc.tile_pool(name="sb", bufs=1))
        ps = ctx.enter_context(tc.psum_pool(name="ps", bufs=1))
        ctx.enter_context(tc.manual_schedule())

        ident = sb.tile([P, P], F32, name="ident")
        warm = sb.tile([P, 16], F32, name="warm")
        lam = sb.tile([P, GROUPS, PACK], BF16, name="lam")
        x_raw = sb.tile([P, X_TILES, K], BF16, name="x_raw")
        a_raw = sb.tile([P, GROUPS, PASSES, PACK, GROUP], BF16, name="a_raw")
        x_stage = sb.tile([P, QUARTERS - 1, PASSES * UNIT_COLS], BF16, name="x_stage", align_bytes=64)
        a_stage = sb.tile([P, 2, PASS_COLS], BF16, name="a_stage", align_bytes=64)
        g_stage = sb.tile([P, 2 * PASS_COLS], BF16, name="g_stage", align_bytes=64)
        x_codes = sb.tile([P, QUARTERS, PASSES * UNIT_M], U32, name="x_codes", align_bytes=64)
        x_scales = sb.tile([P, QUARTERS, PASSES * UNIT_M], U8, name="x_scales", align_bytes=64)
        a_codes = sb.tile([P, GROUPS, PASSES, GROUP], U32, name="a_codes", align_bytes=64)
        a_scales = sb.tile([P, GROUPS, PASSES, GROUP], U8, name="a_scales", align_bytes=64)
        y_codes = sb.tile([P, GROUPS * M], U32, name="y_codes", align_bytes=64)
        y_scales = sb.tile([P, GROUPS * M], U8, name="y_scales", align_bytes=64)
        e_t = sb.tile([P, RING, BANK], F32, name="e_t")
        r_t = sb.tile([P, RING, BANK], F32, name="r_t")
        u_t = sb.tile([P, RING, BANK], F32, name="u_t")
        g_t = sb.tile([P, RING, BANK], F32, name="g_t")
        y_t = sb.tile([P, UNITS, PACK, UNIT_M], F32, name="y_t")
        o_t = sb.tile([P, OUT_RING, BANK], F32, name="o_t")
        c_bank = [ps.tile([P, BANK], F32, name="c_bank%d" % b) for b in range(C_BANKS)]
        t_bank = [ps.tile([P, BANK], F32, name="t_bank%d" % b) for b in range(T_BANKS)]

        lower, upper = g_stage[:, 0:PASS_COLS], g_stage[:, PASS_COLS : 2 * PASS_COLS]

        def g_units(first, last):
            return g_stage[:, first * UNIT_COLS : last * UNIT_COLS]

        def copy(engine, out, in_):
            if engine == "scalar":
                nc.scalar.copy(out=out, in_=in_)
            elif engine == "vector":
                nc.vector.tensor_copy(out=out, in_=in_)
            else:
                nc.gpsimd.tensor_scalar(out=out, in0=in_, scalar1=1.0, scalar2=1.0, op0=MULT, op1=MULT)

        def quantize(codes, scales, src):
            nc.vector.quantize_mx(out=codes.bitcast(FP8X4), scales=scales, in_=src)


        def load_x(first, last):
            rows = x_rows[first * P : last * P, :]
            nc.sync.dma_start(out=x_raw[:, first:last, :], in_=rows.rearrange("(b p) k -> p b k", p=P))

        def x_stage_of(q):
            return lower if q == QUARTERS - 1 else x_stage[:, q, :]

        def x_bank(b):
            return (t_bank + [c_bank[4], c_bank[3]] + t_bank)[b]

        def turn_x(b):
            words = x_raw[:, b, :].bitcast(F32)
            half = K_PASS // 2
            for j in range(PASSES):
                for h in range(2):
                    col = (2 * j + h) * P
                    nc.tensor.transpose(
                        x_bank(b)[:, col : col + P], words[:, half * j + h : half * (j + 1) : 2], ident[:]
                    )

        def copy_x(engine, b):
            dst = x_stage_of(b // 2).bitcast(F32).rearrange("p (j m h) -> p j m h", j=PASSES, h=2)
            m0 = (b % 2) * P
            copy(
                engine,
                dst[:, :, m0 : m0 + P, :],
                x_bank(b)[:].rearrange("p (j h m) -> p j m h", j=PASSES, h=2),
            )

        def quant_x(q):
            quantize(x_codes[:, q, :], x_scales[:, q, :], x_stage_of(q))


        def load_a(g, j):
            rows = analysis[j * K_PASS : (j + 1) * K_PASS, g * GROUP : (g + 1) * GROUP]
            nc.sync.dma_start(out=a_raw[:, g, j, :, :], in_=rows.rearrange("(p r) n -> p r n", r=PACK))

        def weave_a(engine, g, j, stage, t0=0, t1=PACK):
            src = a_raw[:, g, j, :, :].rearrange("p r (c t) -> p t c r", t=PACK)
            dst = stage.rearrange("p (t c r) -> p t c r", t=PACK, r=PACK)
            copy(engine, dst[:, t0:t1], src[:, t0:t1])

        def quant_a(g, j, stage):
            quantize(a_codes[:, g, j, :], a_scales[:, g, j, :], stage)


        def item(i):
            if i // 2 < UNITS - 1:
                return range(2 * (i % 2), 2 * (i % 2) + 2), 0, UNIT_M
            return range(PACK), (i % 2) * P, P

        def multiply(i):
            g, q = divmod(i // 2, QUARTERS)
            slices, m0, width = item(i)
            for place, t in enumerate(slices):
                for j in range(PASSES):
                    cols = slice(j * UNIT_M + m0, j * UNIT_M + m0 + width)
                    nc.tensor.matmul_mx(
                        out=c_bank[i % C_BANKS][:, place * width : (place + 1) * width],
                        lhsT=a_codes[:, g, j, t * P : (t + 1) * P].bitcast(FP8X4),
                        lhsT_scale=a_scales[:, g, j, t * P : (t + 1) * P],
                        rhs=x_codes[:, q, cols].bitcast(FP8X4),
                        rhs_scale=x_scales[:, q, cols],
                        start=(j == 0),
                        stop=(j == PASSES - 1),
                    )

        def square_c(i):
            nc.scalar.activation(out=e_t[:, i % RING, :], in_=c_bank[i % C_BANKS][:], func=ACT.Square)

        def rsqrt(i):
            g = i // (2 * QUARTERS)
            slices, m0, width = item(i)
            for place, t in enumerate(slices):
                cols = slice(place * width, (place + 1) * width)
                nc.scalar.activation(
                    out=r_t[:, i % RING, cols],
                    in_=e_t[:, i % RING, cols],
                    func=ACT.Abs_reciprocal_sqrt,
                    bias=lam[:, g, t : t + 1],
                )

        def ratio(i):
            nc.vector.tensor_tensor(
                out=u_t[:, i % RING, :], in0=c_bank[i % C_BANKS][:], in1=r_t[:, i % RING, :], op=MULT
            )

        def gain(i):
            nc.scalar.activation(out=g_t[:, i % RING, :], in_=u_t[:, i % RING, :], func=ACT.Square)

        def shrink(i):
            slices, m0, width = item(i)
            nc.vector.tensor_tensor(
                out=y_t[:, i // 2, slices[0] : slices[-1] + 1, m0 : m0 + width],
                in0=c_bank[i % C_BANKS][:].rearrange("p (t m) -> p t m", m=width),
                in1=g_t[:, i % RING, :].rearrange("p (t m) -> p t m", m=width),
                op=MULT,
            )


        def out_bank(block):
            if block >= ITEMS - 4:
                return c_bank[(block - 1) % C_BANKS]
            return t_bank[block % T_BANKS]

        def turn_y(block):
            unit, half = divmod(block, 2)
            for t in range(PACK):
                nc.tensor.transpose(
                    out_bank(block)[:, t * P : (t + 1) * P], y_t[:, unit, t, half * P : (half + 1) * P], ident[:]
                )

        def store_y(engine, block):
            g, b = divmod(block, X_TILES)
            dst = o_t[:, block % OUT_RING, :]
            copy(
                engine,
                dst.rearrange("m (p t) -> m p t", t=PACK),
                out_bank(block)[:].rearrange("m (t p) -> m p t", t=PACK),
            )
            nc.sync.dma_start(out=y_rows[b * P : (b + 1) * P, g * GROUP : (g + 1) * GROUP], in_=dst)


        def round_y(engine, first, last, stage):
            copy(
                engine,
                stage.rearrange("p (u m t) -> p u m t", m=UNIT_M, t=PACK),
                y_t[:, first:last].rearrange("p u t m -> p u m t"),
            )

        def quant_y(first, last, stage):
            cols = slice(first * UNIT_M, last * UNIT_M)
            quantize(y_codes[:, cols], y_scales[:, cols], stage)

        def store_words(first, last):
            for g in range(first // QUARTERS, (last - 1) // QUARTERS + 1):
                lo, hi = max(first, g * QUARTERS), min(last, (g + 1) * QUARTERS)
                nc.sync.dma_start(
                    out=words_hbm[g, :, (lo - g * QUARTERS) * UNIT_M : (hi - g * QUARTERS) * UNIT_M],
                    in_=y_codes[:, lo * UNIT_M : hi * UNIT_M].bitcast(I32),
                )

        def store_scales(first, last):
            plane = y_scales[:].bitcast(I32).rearrange("p (g w) -> p g w", g=GROUPS)
            for quad in range(4):
                nc.sync.dma_start(
                    out=scales_hbm[first:last, 4 * quad : 4 * quad + 4, :].rearrange("g r w -> r g w"),
                    in_=plane[32 * quad : 32 * quad + 4, first:last, :],
                )


        with nc.allow_non_contiguous_dma(reason="four thresholds to a partition and group"):
            nc.scalar.dma_start(out=lam[:], in_=lam_sq.rearrange("(g p t) -> p g t", p=P, t=PACK))
        nc.vector.memset(warm[:, 0:1], 1.0)
        nc.scalar.activation(out=warm[:, 8:9], in_=warm[:, 0:1], func=ACT.Abs_reciprocal_sqrt)
        load_a(0, 0)
        load_a(0, 1)
        load_x(0, 1)
        load_x(1, 2)
        load_x(2, 4)
        load_x(4, 6)
        load_a(1, 0)
        load_x(6, 8)
        load_a(1, 1)
        for g in range(2, GROUPS):
            for j in range(PASSES):
                load_a(g, j)
        make_identity(nc, ident[:])

        weave_a("vector", 0, 0, a_stage[:, 0, :])
        weave_a("vector", 0, 1, a_stage[:, 1, :], 0, 2)
        weave_a("scalar", 0, 1, a_stage[:, 1, :], 2, 4)
        quant_a(0, 0, a_stage[:, 0, :])
        quant_a(0, 1, a_stage[:, 1, :])
        for b in range(6):
            turn_x(b)
            copy_x("scalar", b)
            if b in (1, 3):
                quant_x(b // 2)
        multiply(0)
        multiply(1)
        weave_a("vector", 1, 0, a_stage[:, 0, :])
        quant_x(2)
        turn_x(6)
        turn_x(7)
        square_c(0)
        square_c(1)
        rsqrt(0)
        rsqrt(1)
        copy_x("scalar", 6)
        copy_x("vector", 7)
        quant_a(1, 0, a_stage[:, 0, :])
        quant_x(3)
        weave_a("gpsimd", 1, 1, lower)
        weave_a("gpsimd", 2, 0, upper)

        for i in (2, 3, 4):
            multiply(i)
        square_c(2)
        square_c(3)
        rsqrt(2)
        square_c(4)
        for i in range(3):
            ratio(i)
        gain(0)
        rsqrt(3)
        gain(1)
        gain(2)
        shrink(0)
        multiply(5)
        shrink(1)
        multiply(6)
        ratio(3)

        first_step, last_step = 5, ITEMS - 3
        first_hand_over, period = 7, 4

        def hand_over(n):
            if n == 0:
                quant_a(1, 1, lower)
                multiply(8)
                quant_a(2, 0, upper)
                weave_a("gpsimd", 2, 1, upper)
                round_y("gpsimd", 0, 1, g_units(0, 1))
            elif n == 1:
                quant_a(2, 1, upper)
                quant_y(0, 1, g_units(0, 1))
                store_words(0, 1)
                weave_a("gpsimd", 3, 0, lower)
                round_y("gpsimd", 1, 2, g_units(2, 3))
            elif n == 2:
                quant_a(3, 0, lower)
                quant_y(1, 2, g_units(2, 3))
                store_words(1, 2)
                weave_a("gpsimd", 3, 1, upper)
                round_y("gpsimd", 2, 3, g_units(0, 1))
            elif n == 3:
                quant_a(3, 1, upper)
                quant_y(2, 3, g_units(0, 1))
                store_words(2, 3)
                round_y("gpsimd", 3, 6, g_units(0, 3))
            else:
                staged = 3 * (n - 3)
                quant_y(staged, staged + 2, g_units(0, 2))
                quant_y(staged + 2, staged + 3, g_units(2, 3))
                store_words(staged, staged + 3)
                round_y("gpsimd", staged + 3, staged + 6, g_units(0, 3))

        for s in range(first_step, last_step + 1):
            n, phase = divmod(s - first_hand_over, period)
            vector_quantises = n >= 0 and phase == 0
            if vector_quantises:
                hand_over(n)
            if s % 2 == 1:
                turn_y(s - 5)
                turn_y(s - 4)
            block = s - 6
            if block >= 0 and not vector_quantises:
                store_y("vector", block)
            rsqrt(s - 1)
            square_c(s)
            gain(s - 2)
            if vector_quantises:
                store_y("scalar", block)
            shrink(s - 3)
            ratio(s - 1)
            if s != first_hand_over - 1:
                multiply(s + 2)

        store_y("vector", 24)
        rsqrt(29)
        square_c(30)
        gain(28)
        shrink(27)
        quant_y(11, 12, g_units(2, 3))
        quant_y(9, 11, g_units(0, 2))
        round_y("gpsimd", 12, 14, g_units(0, 2))
        ratio(29)
        turn_y(26)
        store_y("scalar", 25)
        store_words(9, 12)
        store_scales(0, 3)
        turn_y(27)
        rsqrt(30)
        square_c(31)
        gain(29)
        rsqrt(31)
        shrink(28)
        ratio(30)
        shrink(29)
        round_y("gpsimd", 14, 15, g_units(2, 3))
        turn_y(28)
        turn_y(29)
        store_y("scalar", 26)
        gain(30)
        ratio(31)
        store_y("vector", 27)
        gain(31)
        shrink(30)
        turn_y(30)
        shrink(31)
        turn_y(31)
        store_y("scalar", 28)
        store_y("scalar", 29)
        quant_y(12, 14, g_units(0, 2))
        store_words(12, 14)
        round_y("scalar", 15, 16, g_units(3, 4))
        store_y("vector", 30)
        store_y("vector", 31)
        quant_y(14, 16, g_units(2, 4))
        store_scales(3, 4)
        store_words(14, 16)
